import numpy as np, ml_dtypes
CORES = [13,21,141,149]
N = 4
R = 512
def setup_inputs(rng):
    m = (rng.standard_normal((N, 128, 128), dtype=np.float32) / 11).astype(ml_dtypes.bfloat16)
    q = rng.standard_normal((128, R), dtype=np.float32).astype(ml_dtypes.bfloat16)
    return {"m": m, "mt": m.transpose(0, 2, 1).copy(), "q": np.broadcast_to(q, (N, 128, R)).copy()}
def setup_inputs_big(rng):
    d = setup_inputs(rng)
    for k in ("m", "mt", "q"): d[k] = (d[k].astype(np.float32) * 1024.0).astype(d[k].dtype)
    return d
def setup_inputs_small(rng):
    d = setup_inputs(rng)
    for k in ("m", "mt", "q"): d[k] = (d[k].astype(np.float32) * (1 / 1024.0)).astype(d[k].dtype)
    return d
def setup_inputs_apart(rng):
    d = setup_inputs(rng)
    f = (10.0 ** rng.permutation(np.linspace(-1.5, 1.5, N))).astype(np.float32).reshape(N, 1, 1)
    for k in ("m", "mt"): d[k] = (d[k].astype(np.float32) * f).astype(d[k].dtype)
    return d
def reference(m, mt, q):
    M, MT, Q = m.astype(np.float64), mt.astype(np.float64), q.astype(np.float64)
    p = sum(MT[j].T @ Q[j] for j in range(N))
    q2 = sum(M[j].T @ p for j in range(N))
    return {"p": np.broadcast_to(p.astype(ml_dtypes.bfloat16), (N, 128, R)), "q2": np.broadcast_to(q2.astype(ml_dtypes.bfloat16), (N, 128, R))}

@@ -1,0 +1,188 @@
+from concourse.bass import DstId, RemoteDMATransfer
+
+D = 128
+R = 512
+HALF = R // 2
+
+N_STAGE = 4
+
+SCRATCH = {
+    "stage": ("dram", [D, D], "bfloat16"),
+    "mt_sb": ("sbuf", [D, D], "bfloat16"),
+    "peer": ("sbuf", [D, D], "bfloat16"),
+    "cross": ("sbuf", [D, D], "bfloat16"),
+    "ident": ("sbuf", [D, D], "bfloat16"),
+    "q_sb": ("sbuf", [D, R], "bfloat16"),
+    "s_sb": ("sbuf", [D, D], "bfloat16"),
+    "p_sb": ("sbuf", [D, R], "bfloat16"),
+    "q2_sb": ("sbuf", [D, R], "bfloat16"),
+    "ps_s": ("psum", [D, 512], "float32"),
+    "ps_p0": ("psum", [D, 512], "float32"),
+    "ps_p1": ("psum", [D, 512], "float32"),
+    "ps_q0": ("psum", [D, 512], "float32"),
+    "ps_q1": ("psum", [D, 512], "float32"),
+    "hland": ("dram", [2, D, D], "bfloat16"),
+    "zcol": ("sbuf", [D, D + 1], "bfloat16"),
+    "skew": ("dram", [D + 1, D], "bfloat16"),
+}
+SEMAPHORES = [
+    "ld_stage", "ld_mt", "ld_q",
+    "sent",
+    "landed",
+    "peer_in", "cross_in", "ident_in",
+    "fill", "skewed",
+    "mm_s", "mm_p0", "mm_p1", "mm_q0", "mm_q1",
+    "cp_s", "cp_p0", "cp_p1", "cp_q0", "cp_q1",
+    "st_sync", "st_scal",
+]
+
+
+def _bits(mask):
+    return [e for e in range(mask.bit_length()) if (mask >> e) & 1]
+
+
+def _pick(mask, n):
+    bits = _bits(mask)
+    out = 0
+    for e in bits[:: len(bits) // n][:n]:
+        out |= 1 << e
+    return out
+
+
+def _count(mask):
+    return len(_bits(mask))
+
+
+def _plan(T, topo):
+    ranks = list(T.cores)
+    n_cores = (max(topo.host(r) for r in ranks) + 1) * topo.CORES_PER_HOST
+    plan = {}
+    for r in ranks:
+        group = [s for s in ranks if s == r or topo.may_write(r, s)]
+        far = [s for s in ranks if s not in group]
+        helper = [c for c in range(n_cores)
+                  if topo.host(c) == topo.host(r) and topo.chip(c) == topo.chip(r) and topo.die(c) == topo.die(r)
+                  and c not in ranks and all(topo.may_write(c, f) for f in far)][0]
+        plan[r] = {"group": group, "helper": helper, "target": far[group.index(r)]}
+    return plan
+
+
+def _stage_masks(core, plan, topo):
+    helpers = [plan[s]["helper"] for s in plan[core]["group"]]
+    helpers.sort(key=lambda h: _count(topo.mask(core, h)))
+    used, masks = 0, {}
+    narrow = topo.mask(core, helpers[0])
+    for h in helpers:
+        free = topo.mask(core, h) & ~used
+        if h != helpers[0] and _count(free & ~narrow) >= N_STAGE:
+            free &= ~narrow
+        masks[h] = _pick(free, N_STAGE)
+        used |= masks[h]
+    return masks
+
+
+def _rank(g, core, T, topo, plan):
+    sem = T.sem
+    group = plan[core]["group"]
+    slot = group.index(core)
+    partner = [s for s in group if s != core][0]
+    feeder = [plan[s]["helper"] for s in plan if plan[s]["target"] == core][0]
+    helper = plan[core]["helper"]
+
+    g.sync.dma_start(T.stage[:], T.mt[:]).then_inc(sem.ld_stage, 16)
+    g.sync.dma_start(T.mt_sb[:], T.mt[:]).then_inc(sem.ld_mt, 16)
+    g.sync.dma_start(T.q_sb[:], T.q[:]).then_inc(sem.ld_q, 16)
+
+    masks = _stage_masks(core, plan, topo)
+    transfers, sent = [], 0
+    for h, mask in masks.items():
+        rid, pid = topo.addr(h, core)
+        transfers.append(RemoteDMATransfer(dst_ids=[DstId(rid=rid, pnc=pid)], dma_engine_mask=mask,
+                                           remote_sem=sem.landed, src=T.stage[:], dst=T.hland[slot]))
+        sent += _count(mask)
+    g.wait_ge(sem.ld_stage, 16)
+    g.remote_dma_fused(transfers, local_sem=sem.sent)
+    rid, pid = topo.addr(partner, core)
+    pmask = masks[plan[partner]["helper"]]
+    g.remote_dma(out_ap=T.peer[:], in_ap=T.stage[:], remote_sem=sem.peer_in, local_sem=sem.sent,
+                 pid=pid, routing_id=rid, dma_engine_mask=pmask)
+    sent += _count(pmask)
+    g.wait_ge(sem.sent, sent)
+
+    t, v = g.tensor, g.vector
+    q0, q1 = T.q_sb[:, 0:HALF], T.q_sb[:, HALF:R]
+    pp0, pp1, pps = T.ps_p0[:, 0:HALF], T.ps_p1[:, 0:HALF], T.ps_s[:, 0:D]
+
+    def term(lhsT, first, last):
+        t.matmul(pps, lhsT, T.ident[:], start=first, stop=last).then_inc(sem.mm_s, 1)
+        t.matmul(pp0, lhsT, q0, start=first, stop=last).then_inc(sem.mm_p0, 1)
+        t.matmul(pp1, lhsT, q1, start=first, stop=last).then_inc(sem.mm_p1, 1)
+
+    t.wait_ge(sem.ld_mt, 16)
+    t.wait_ge(sem.ld_q, 16)
+    t.wait_ge(sem.ident_in, _count(topo.mask(helper, plan[core]["target"])))
+    term(T.mt_sb[:], True, False)
+    t.wait_ge(sem.peer_in, _count(_stage_masks(partner, plan, topo)[helper]))
+    term(T.peer[:], False, False)
+    t.wait_ge(sem.cross_in, _count(topo.mask(feeder, core)))
+    term(T.cross[:], False, True)
+    t.wait_ge(sem.cp_s, 1)
+    t.wait_ge(sem.cp_p0, 1)
+    t.matmul(T.ps_q0[:, 0:HALF], T.s_sb[:], T.p_sb[:, 0:HALF], start=True, stop=True).then_inc(sem.mm_q0, 1)
+    t.wait_ge(sem.cp_p1, 1)
+    t.matmul(T.ps_q1[:, 0:HALF], T.s_sb[:], T.p_sb[:, HALF:R], start=True, stop=True).then_inc(sem.mm_q1, 1)
+
+    v.wait_ge(sem.mm_s, 3)
+    v.tensor_copy(T.s_sb[:], pps).then_inc(sem.cp_s, 1)
+    v.wait_ge(sem.mm_p0, 3)
+    v.tensor_copy(T.p_sb[:, 0:HALF], pp0).then_inc(sem.cp_p0, 1)
+    v.wait_ge(sem.mm_p1, 3)
+    v.tensor_copy(T.p_sb[:, HALF:R], pp1).then_inc(sem.cp_p1, 1)
+    v.wait_ge(sem.mm_q0, 1)
+    v.tensor_copy(T.q2_sb[:, 0:HALF], T.ps_q0[:, 0:HALF]).then_inc(sem.cp_q0, 1)
+    v.wait_ge(sem.mm_q1, 1)
+    v.tensor_copy(T.q2_sb[:, HALF:R], T.ps_q1[:, 0:HALF]).then_inc(sem.cp_q1, 1)
+
+    g.scalar.wait_ge(sem.cp_p0, 1)
+    g.scalar.dma_start(T.p[:, 0:HALF], T.p_sb[:, 0:HALF]).then_inc(sem.st_scal, 16)
+    g.scalar.wait_ge(sem.cp_q0, 1)
+    g.scalar.dma_start(T.q2[:, 0:HALF], T.q2_sb[:, 0:HALF]).then_inc(sem.st_scal, 16)
+    g.scalar.wait_ge(sem.st_scal, 32)
+    g.sync.wait_ge(sem.cp_p1, 1)
+    g.sync.dma_start(T.p[:, HALF:R], T.p_sb[:, HALF:R]).then_inc(sem.st_sync, 16)
+    g.sync.wait_ge(sem.cp_q1, 1)
+    g.sync.dma_start(T.q2[:, HALF:R], T.q2_sb[:, HALF:R]).then_inc(sem.st_sync, 16)
+    g.sync.wait_ge(sem.st_sync, 32)
+
+
+def _helper(g, core, T, topo, plan, rank):
+    sem = T.sem
+    target = plan[rank]["target"]
+    mask = topo.mask(core, target)
+
+    g.vector.memset(T.zcol[:, 1:D + 1], 0.0).then_inc(sem.fill, 1)
+    g.vector.memset(T.zcol[:, 0:1], 1.0).then_inc(sem.fill, 1)
+    g.sync.wait_ge(sem.fill, 2)
+    g.sync.dma_start(T.skew[:], T.zcol[:]).then_inc(sem.skewed, 16)
+    g.wait_ge(sem.skewed, 16)
+    rid, pid = topo.addr(rank, core)
+    g.remote_dma(out_ap=T.ident[:], in_ap=T.skew[0:D, :], remote_sem=sem.ident_in, local_sem=sem.sent,
+                 pid=pid, routing_id=rid, dma_engine_mask=mask & topo.mask(core, rank))
+
+    landed = sum(_count(_stage_masks(s, plan, topo)[core]) for s in plan[rank]["group"])
+    g.wait_ge(sem.landed, landed)
+    rid, pid = topo.addr(target, core)
+    g.remote_dma_fused([RemoteDMATransfer(dst_ids=[DstId(rid=rid, pnc=pid)], dma_engine_mask=mask,
+                                          remote_sem=sem.cross_in, srcs=[T.hland[0], T.hland[1]], dsts=[T.cross[:]],
+                                          alu_op=1)], local_sem=sem.sent)
+    g.wait_ge(sem.sent, _count(mask & topo.mask(core, rank)) + _count(mask))
+
+
+def rank_program(g, core, T, topo):
+    plan = _plan(T, topo)
+    if core in plan:
+        _rank(g, core, T, topo, plan)
+        return
+    for rank in plan:
+        if plan[rank]["helper"] == core:
+            _helper(g, core, T, topo, plan, rank)

@@ -1,16 +1,17 @@
 from concourse.bass import DstId, RemoteDMATransfer
+from concourse.mybir import AluOpType
 
 D = 128
 R = 512
 HALF = R // 2
-
-N_STAGE = 4
+IP = 8
 
 SCRATCH = {
     "stage": ("dram", [D, D], "bfloat16"),
     "mt_sb": ("sbuf", [D, D], "bfloat16"),
     "peer": ("sbuf", [D, D], "bfloat16"),
     "cross": ("sbuf", [D, D], "bfloat16"),
+    "index": ("sbuf", [D, D], "bfloat16"),
     "ident": ("sbuf", [D, D], "bfloat16"),
     "q_sb": ("sbuf", [D, R], "bfloat16"),
     "s_sb": ("sbuf", [D, D], "bfloat16"),
@@ -22,15 +23,14 @@ SCRATCH = {
     "ps_q0": ("psum", [D, 512], "float32"),
     "ps_q1": ("psum", [D, 512], "float32"),
     "hland": ("dram", [2, D, D], "bfloat16"),
-    "zcol": ("sbuf", [D, D + 1], "bfloat16"),
-    "skew": ("dram", [D + 1, D], "bfloat16"),
+    "icols": ("sbuf", [D, D], "bfloat16"),
 }
 SEMAPHORES = [
     "ld_stage", "ld_mt", "ld_q",
     "sent",
     "landed",
-    "peer_in", "cross_in", "ident_in",
-    "fill", "skewed",
+    "peer_in", "cross_in", "index_in",
+    "made", "compared",
     "mm_s", "mm_p0", "mm_p1", "mm_q0", "mm_q1",
     "cp_s", "cp_p0", "cp_p1", "cp_q0", "cp_q1",
     "st_sync", "st_scal",
@@ -41,10 +41,9 @@ def _bits(mask):
     return [e for e in range(mask.bit_length()) if (mask >> e) & 1]
 
 
-def _pick(mask, n):
-    bits = _bits(mask)
+def _mask(bits):
     out = 0
-    for e in bits[:: len(bits) // n][:n]:
+    for e in bits:
         out |= 1 << e
     return out
 
@@ -63,39 +62,52 @@ def _plan(T, topo):
         helper = [c for c in range(n_cores)
                   if topo.host(c) == topo.host(r) and topo.chip(c) == topo.chip(r) and topo.die(c) == topo.die(r)
                   and c not in ranks and all(topo.may_write(c, f) for f in far)][0]
-        plan[r] = {"group": group, "helper": helper, "target": far[group.index(r)]}
+        plan[r] = {"group": group, "helper": helper, "target": far[group.index(r)],
+                   "partner": [s for s in group if s != r][0]}
     return plan
 
 
-def _stage_masks(core, plan, topo):
-    helpers = [plan[s]["helper"] for s in plan[core]["group"]]
-    helpers.sort(key=lambda h: _count(topo.mask(core, h)))
-    used, masks = 0, {}
-    narrow = topo.mask(core, helpers[0])
-    for h in helpers:
-        free = topo.mask(core, h) & ~used
-        if h != helpers[0] and _count(free & ~narrow) >= N_STAGE:
-            free &= ~narrow
-        masks[h] = _pick(free, N_STAGE)
-        used |= masks[h]
-    return masks
+def _lanes(rank, plan, topo):
+    out = topo.mask(rank, plan[rank]["partner"])
+    bits = _bits(out)
+    stay = _bits(topo.mask(rank, plan[rank]["helper"]) & ~out)
+    return {"away": _mask(bits[0::2]), "index": _mask(bits[1::2]), "home": _mask(stay[0::2])}
+
+
+def _helper_lanes(rank, plan, topo):
+    h = plan[rank]["helper"]
+    fold = topo.mask(h, plan[rank]["target"])
+    return {"fold": fold, "index": fold & topo.mask(h, rank)}
+
+
+def _send_index_columns(g, core, T, topo, first, width, dst, mask):
+    sem = T.sem
+    tile = T.icols[:, 0:width]
+    g.iota(tile, [[-1, width]], -first, 1, allow_small_or_imprecise_dtypes=True).then_inc(sem.made, 1)
+    g.wait_ge(sem.made, 1)
+    rid, pid = topo.addr(dst, core)
+    g.remote_dma(out_ap=T.index[:, first:first + width], in_ap=tile, remote_sem=sem.index_in, local_sem=sem.sent,
+                 pid=pid, routing_id=rid, dma_engine_mask=mask)
+    return _count(mask)
 
 
 def _rank(g, core, T, topo, plan):
     sem = T.sem
     group = plan[core]["group"]
     slot = group.index(core)
-    partner = [s for s in group if s != core][0]
-    feeder = [plan[s]["helper"] for s in plan if plan[s]["target"] == core][0]
+    partner = plan[core]["partner"]
+    feeder = [s for s in plan if plan[s]["target"] == core][0]
     helper = plan[core]["helper"]
+    lanes = _lanes(core, plan, topo)
 
     g.sync.dma_start(T.stage[:], T.mt[:]).then_inc(sem.ld_stage, 16)
     g.sync.dma_start(T.mt_sb[:], T.mt[:]).then_inc(sem.ld_mt, 16)
     g.sync.dma_start(T.q_sb[:], T.q[:]).then_inc(sem.ld_q, 16)
 
-    masks = _stage_masks(core, plan, topo)
-    transfers, sent = [], 0
-    for h, mask in masks.items():
+    sent = _send_index_columns(g, core, T, topo, D - IP, IP, partner, lanes["index"])
+
+    transfers = []
+    for h, mask in ((plan[partner]["helper"], lanes["away"]), (helper, lanes["home"])):
         rid, pid = topo.addr(h, core)
         transfers.append(RemoteDMATransfer(dst_ids=[DstId(rid=rid, pnc=pid)], dma_engine_mask=mask,
                                            remote_sem=sem.landed, src=T.stage[:], dst=T.hland[slot]))
@@ -103,35 +115,41 @@ def _rank(g, core, T, topo, plan):
     g.wait_ge(sem.ld_stage, 16)
     g.remote_dma_fused(transfers, local_sem=sem.sent)
     rid, pid = topo.addr(partner, core)
-    pmask = masks[plan[partner]["helper"]]
     g.remote_dma(out_ap=T.peer[:], in_ap=T.stage[:], remote_sem=sem.peer_in, local_sem=sem.sent,
-                 pid=pid, routing_id=rid, dma_engine_mask=pmask)
-    sent += _count(pmask)
+                 pid=pid, routing_id=rid, dma_engine_mask=lanes["away"])
+    sent += _count(lanes["away"])
     g.wait_ge(sem.sent, sent)
 
     t, v = g.tensor, g.vector
     q0, q1 = T.q_sb[:, 0:HALF], T.q_sb[:, HALF:R]
     pp0, pp1, pps = T.ps_p0[:, 0:HALF], T.ps_p1[:, 0:HALF], T.ps_s[:, 0:D]
 
-    def term(lhsT, first, last):
+    def s_term(lhsT, first, last):
         t.matmul(pps, lhsT, T.ident[:], start=first, stop=last).then_inc(sem.mm_s, 1)
+
+    def p_term(lhsT, first, last):
         t.matmul(pp0, lhsT, q0, start=first, stop=last).then_inc(sem.mm_p0, 1)
         t.matmul(pp1, lhsT, q1, start=first, stop=last).then_inc(sem.mm_p1, 1)
 
     t.wait_ge(sem.ld_mt, 16)
     t.wait_ge(sem.ld_q, 16)
-    t.wait_ge(sem.ident_in, _count(topo.mask(helper, plan[core]["target"])))
-    term(T.mt_sb[:], True, False)
-    t.wait_ge(sem.peer_in, _count(_stage_masks(partner, plan, topo)[helper]))
-    term(T.peer[:], False, False)
-    t.wait_ge(sem.cross_in, _count(topo.mask(feeder, core)))
-    term(T.cross[:], False, True)
+    p_term(T.mt_sb[:], True, False)
+    t.wait_ge(sem.peer_in, _count(_lanes(partner, plan, topo)["away"]))
+    p_term(T.peer[:], False, False)
+    t.wait_ge(sem.compared, 1)
+    s_term(T.mt_sb[:], True, False)
+    s_term(T.peer[:], False, False)
+    t.wait_ge(sem.cross_in, _count(_helper_lanes(feeder, plan, topo)["fold"]))
+    s_term(T.cross[:], False, True)
+    p_term(T.cross[:], False, True)
     t.wait_ge(sem.cp_s, 1)
     t.wait_ge(sem.cp_p0, 1)
     t.matmul(T.ps_q0[:, 0:HALF], T.s_sb[:], T.p_sb[:, 0:HALF], start=True, stop=True).then_inc(sem.mm_q0, 1)
     t.wait_ge(sem.cp_p1, 1)
     t.matmul(T.ps_q1[:, 0:HALF], T.s_sb[:], T.p_sb[:, HALF:R], start=True, stop=True).then_inc(sem.mm_q1, 1)
 
+    v.wait_ge(sem.index_in, _count(_helper_lanes(core, plan, topo)["index"]) + _count(_lanes(partner, plan, topo)["index"]))
+    v.tensor_scalar(T.ident[:], T.index[:], 0.0, None, AluOpType.is_equal).then_inc(sem.compared, 1)
     v.wait_ge(sem.mm_s, 3)
     v.tensor_copy(T.s_sb[:], pps).then_inc(sem.cp_s, 1)
     v.wait_ge(sem.mm_p0, 3)
@@ -158,24 +176,17 @@ def _rank(g, core, T, topo, plan):
 def _helper(g, core, T, topo, plan, rank):
     sem = T.sem
     target = plan[rank]["target"]
-    mask = topo.mask(core, target)
+    lanes = _helper_lanes(rank, plan, topo)
 
-    g.vector.memset(T.zcol[:, 1:D + 1], 0.0).then_inc(sem.fill, 1)
-    g.vector.memset(T.zcol[:, 0:1], 1.0).then_inc(sem.fill, 1)
-    g.sync.wait_ge(sem.fill, 2)
-    g.sync.dma_start(T.skew[:], T.zcol[:]).then_inc(sem.skewed, 16)
-    g.wait_ge(sem.skewed, 16)
-    rid, pid = topo.addr(rank, core)
-    g.remote_dma(out_ap=T.ident[:], in_ap=T.skew[0:D, :], remote_sem=sem.ident_in, local_sem=sem.sent,
-                 pid=pid, routing_id=rid, dma_engine_mask=mask & topo.mask(core, rank))
+    sent = _send_index_columns(g, core, T, topo, 0, D - IP, rank, lanes["index"])
 
-    landed = sum(_count(_stage_masks(s, plan, topo)[core]) for s in plan[rank]["group"])
+    landed = sum(_count(_lanes(s, plan, topo)["home" if s == rank else "away"]) for s in plan[rank]["group"])
     g.wait_ge(sem.landed, landed)
     rid, pid = topo.addr(target, core)
-    g.remote_dma_fused([RemoteDMATransfer(dst_ids=[DstId(rid=rid, pnc=pid)], dma_engine_mask=mask,
+    g.remote_dma_fused([RemoteDMATransfer(dst_ids=[DstId(rid=rid, pnc=pid)], dma_engine_mask=lanes["fold"],
                                           remote_sem=sem.cross_in, srcs=[T.hland[0], T.hland[1]], dsts=[T.cross[:]],
                                           alu_op=1)], local_sem=sem.sent)
-    g.wait_ge(sem.sent, _count(mask & topo.mask(core, rank)) + _count(mask))
+    g.wait_ge(sem.sent, sent + _count(lanes["fold"]))
 
 
 def rank_program(g, core, T, topo):

from concourse.bass import DstId, RemoteDMATransfer
from concourse.mybir import AluOpType

D = 128
R = 512
HALF = R // 2
IP = 8

SCRATCH = {
    "stage": ("dram", [D, D], "bfloat16"),
    "mt_sb": ("sbuf", [D, D], "bfloat16"),
    "peer": ("sbuf", [D, D], "bfloat16"),
    "cross": ("sbuf", [D, D], "bfloat16"),
    "index": ("sbuf", [D, D], "bfloat16"),
    "ident": ("sbuf", [D, D], "bfloat16"),
    "q_sb": ("sbuf", [D, R], "bfloat16"),
    "s_sb": ("sbuf", [D, D], "bfloat16"),
    "p_sb": ("sbuf", [D, R], "bfloat16"),
    "q2_sb": ("sbuf", [D, R], "bfloat16"),
    "ps_s": ("psum", [D, 512], "float32"),
    "ps_p0": ("psum", [D, 512], "float32"),
    "ps_p1": ("psum", [D, 512], "float32"),
    "ps_q0": ("psum", [D, 512], "float32"),
    "ps_q1": ("psum", [D, 512], "float32"),
    "hland": ("dram", [2, D, D], "bfloat16"),
    "icols": ("sbuf", [D, D], "bfloat16"),
}
SEMAPHORES = [
    "ld_stage", "ld_mt", "ld_q",
    "sent",
    "landed",
    "peer_in", "cross_in", "index_in",
    "made", "compared",
    "mm_s", "mm_p0", "mm_p1", "mm_q0", "mm_q1",
    "cp_s", "cp_p0", "cp_p1", "cp_q0", "cp_q1",
    "st_sync", "st_scal",
]


def _bits(mask):
    return [e for e in range(mask.bit_length()) if (mask >> e) & 1]


def _mask(bits):
    out = 0
    for e in bits:
        out |= 1 << e
    return out


def _count(mask):
    return len(_bits(mask))


def _plan(T, topo):
    ranks = list(T.cores)
    n_cores = (max(topo.host(r) for r in ranks) + 1) * topo.CORES_PER_HOST
    plan = {}
    for r in ranks:
        group = [s for s in ranks if s == r or topo.may_write(r, s)]
        far = [s for s in ranks if s not in group]
        helper = [c for c in range(n_cores)
                  if topo.host(c) == topo.host(r) and topo.chip(c) == topo.chip(r) and topo.die(c) == topo.die(r)
                  and c not in ranks and all(topo.may_write(c, f) for f in far)][0]
        plan[r] = {"group": group, "helper": helper, "target": far[group.index(r)],
                   "partner": [s for s in group if s != r][0]}
    return plan


def _lanes(rank, plan, topo):
    out = topo.mask(rank, plan[rank]["partner"])
    bits = _bits(out)
    stay = _bits(topo.mask(rank, plan[rank]["helper"]) & ~out)
    return {"away": _mask(bits[0::2]), "index": _mask(bits[1::2]), "home": _mask(stay[0::2])}


def _helper_lanes(rank, plan, topo):
    h = plan[rank]["helper"]
    fold = topo.mask(h, plan[rank]["target"])
    return {"fold": fold, "index": fold & topo.mask(h, rank)}


def _send_index_columns(g, core, T, topo, first, width, dst, mask):
    sem = T.sem
    tile = T.icols[:, 0:width]
    g.iota(tile, [[-1, width]], -first, 1, allow_small_or_imprecise_dtypes=True).then_inc(sem.made, 1)
    g.wait_ge(sem.made, 1)
    rid, pid = topo.addr(dst, core)
    g.remote_dma(out_ap=T.index[:, first:first + width], in_ap=tile, remote_sem=sem.index_in, local_sem=sem.sent,
                 pid=pid, routing_id=rid, dma_engine_mask=mask)
    return _count(mask)


def _rank(g, core, T, topo, plan):
    sem = T.sem
    group = plan[core]["group"]
    slot = group.index(core)
    partner = plan[core]["partner"]
    feeder = [s for s in plan if plan[s]["target"] == core][0]
    helper = plan[core]["helper"]
    lanes = _lanes(core, plan, topo)

    g.sync.dma_start(T.stage[:], T.mt[:]).then_inc(sem.ld_stage, 16)
    g.sync.dma_start(T.mt_sb[:], T.mt[:]).then_inc(sem.ld_mt, 16)
    g.sync.dma_start(T.q_sb[:], T.q[:]).then_inc(sem.ld_q, 16)

    sent = _send_index_columns(g, core, T, topo, D - IP, IP, partner, lanes["index"])

    transfers = []
    for h, mask in ((plan[partner]["helper"], lanes["away"]), (helper, lanes["home"])):
        rid, pid = topo.addr(h, core)
        transfers.append(RemoteDMATransfer(dst_ids=[DstId(rid=rid, pnc=pid)], dma_engine_mask=mask,
                                           remote_sem=sem.landed, src=T.stage[:], dst=T.hland[slot]))
        sent += _count(mask)
    g.wait_ge(sem.ld_stage, 16)
    g.remote_dma_fused(transfers, local_sem=sem.sent)
    rid, pid = topo.addr(partner, core)
    g.remote_dma(out_ap=T.peer[:], in_ap=T.stage[:], remote_sem=sem.peer_in, local_sem=sem.sent,
                 pid=pid, routing_id=rid, dma_engine_mask=lanes["away"])
    sent += _count(lanes["away"])
    g.wait_ge(sem.sent, sent)

    t, v = g.tensor, g.vector
    q0, q1 = T.q_sb[:, 0:HALF], T.q_sb[:, HALF:R]
    pp0, pp1, pps = T.ps_p0[:, 0:HALF], T.ps_p1[:, 0:HALF], T.ps_s[:, 0:D]

    def s_term(lhsT, first, last):
        t.matmul(pps, lhsT, T.ident[:], start=first, stop=last).then_inc(sem.mm_s, 1)

    def p_term(lhsT, first, last):
        t.matmul(pp0, lhsT, q0, start=first, stop=last).then_inc(sem.mm_p0, 1)
        t.matmul(pp1, lhsT, q1, start=first, stop=last).then_inc(sem.mm_p1, 1)

    t.wait_ge(sem.ld_mt, 16)
    t.wait_ge(sem.ld_q, 16)
    p_term(T.mt_sb[:], True, False)
    t.wait_ge(sem.peer_in, _count(_lanes(partner, plan, topo)["away"]))
    p_term(T.peer[:], False, False)
    t.wait_ge(sem.compared, 1)
    s_term(T.mt_sb[:], True, False)
    s_term(T.peer[:], False, False)
    t.wait_ge(sem.cross_in, _count(_helper_lanes(feeder, plan, topo)["fold"]))
    s_term(T.cross[:], False, True)
    p_term(T.cross[:], False, True)
    t.wait_ge(sem.cp_s, 1)
    t.wait_ge(sem.cp_p0, 1)
    t.matmul(T.ps_q0[:, 0:HALF], T.s_sb[:], T.p_sb[:, 0:HALF], start=True, stop=True).then_inc(sem.mm_q0, 1)
    t.wait_ge(sem.cp_p1, 1)
    t.matmul(T.ps_q1[:, 0:HALF], T.s_sb[:], T.p_sb[:, HALF:R], start=True, stop=True).then_inc(sem.mm_q1, 1)

    v.wait_ge(sem.index_in, _count(_helper_lanes(core, plan, topo)["index"]) + _count(_lanes(partner, plan, topo)["index"]))
    v.tensor_scalar(T.ident[:], T.index[:], 0.0, None, AluOpType.is_equal).then_inc(sem.compared, 1)
    v.wait_ge(sem.mm_s, 3)
    v.tensor_copy(T.s_sb[:], pps).then_inc(sem.cp_s, 1)
    v.wait_ge(sem.mm_p0, 3)
    v.tensor_copy(T.p_sb[:, 0:HALF], pp0).then_inc(sem.cp_p0, 1)
    v.wait_ge(sem.mm_p1, 3)
    v.tensor_copy(T.p_sb[:, HALF:R], pp1).then_inc(sem.cp_p1, 1)
    v.wait_ge(sem.mm_q0, 1)
    v.tensor_copy(T.q2_sb[:, 0:HALF], T.ps_q0[:, 0:HALF]).then_inc(sem.cp_q0, 1)
    v.wait_ge(sem.mm_q1, 1)
    v.tensor_copy(T.q2_sb[:, HALF:R], T.ps_q1[:, 0:HALF]).then_inc(sem.cp_q1, 1)

    g.scalar.wait_ge(sem.cp_p0, 1)
    g.scalar.dma_start(T.p[:, 0:HALF], T.p_sb[:, 0:HALF]).then_inc(sem.st_scal, 16)
    g.scalar.wait_ge(sem.cp_q0, 1)
    g.scalar.dma_start(T.q2[:, 0:HALF], T.q2_sb[:, 0:HALF]).then_inc(sem.st_scal, 16)
    g.scalar.wait_ge(sem.st_scal, 32)
    g.sync.wait_ge(sem.cp_p1, 1)
    g.sync.dma_start(T.p[:, HALF:R], T.p_sb[:, HALF:R]).then_inc(sem.st_sync, 16)
    g.sync.wait_ge(sem.cp_q1, 1)
    g.sync.dma_start(T.q2[:, HALF:R], T.q2_sb[:, HALF:R]).then_inc(sem.st_sync, 16)
    g.sync.wait_ge(sem.st_sync, 32)


def _helper(g, core, T, topo, plan, rank):
    sem = T.sem
    target = plan[rank]["target"]
    lanes = _helper_lanes(rank, plan, topo)

    sent = _send_index_columns(g, core, T, topo, 0, D - IP, rank, lanes["index"])

    landed = sum(_count(_lanes(s, plan, topo)["home" if s == rank else "away"]) for s in plan[rank]["group"])
    g.wait_ge(sem.landed, landed)
    rid, pid = topo.addr(target, core)
    g.remote_dma_fused([RemoteDMATransfer(dst_ids=[DstId(rid=rid, pnc=pid)], dma_engine_mask=lanes["fold"],
                                          remote_sem=sem.cross_in, srcs=[T.hland[0], T.hland[1]], dsts=[T.cross[:]],
                                          alu_op=1)], local_sem=sem.sent)
    g.wait_ge(sem.sent, sent + _count(lanes["fold"]))


def rank_program(g, core, T, topo):
    plan = _plan(T, topo)
    if core in plan:
        _rank(g, core, T, topo, plan)
        return
    for rank in plan:
        if plan[rank]["helper"] == core:
            _helper(g, core, T, topo, plan, rank)
